import numpy as np
import ml_dtypes


def mxq(x, axis, fmt="e4m3"):
    dtype, down = {"e4m3": (ml_dtypes.float8_e4m3fn, 7), "e5m2": (ml_dtypes.float8_e5m2, 14)}[fmt]
    v = np.moveaxis(np.asarray(x, np.float32).astype(ml_dtypes.bfloat16).astype(np.float64), axis, -1)
    blocks = v.reshape(v.shape[:-1] + (-1, 32))
    amax = np.abs(blocks).max(-1, keepdims=True)
    byte = np.maximum(np.where(amax > 0, np.frexp(amax)[1] - 1 + 127, 0) - down, 1)
    scale = np.exp2(byte - 127.0)
    codes = (blocks / scale).astype(np.float32).astype(dtype).astype(np.float64)
    return np.moveaxis((codes * scale).reshape(v.shape), -1, axis)


WIDE = False


def mx_kscale(k):
    if not WIDE:
        return np.ones(k)
    levels = np.array([10, -10, 5, -5, 0])
    if k % 512:
        return np.exp2(np.random.permutation(np.resize(levels, k // 32))).repeat(32)
    a = np.empty((k // 512, 16))
    for p in range(k // 512):
        a[p, :8] = np.random.permutation(np.resize(levels, 8))
        for g in range(8):
            far = levels[np.abs(levels - a[p, g]) >= 10]
            a[p, g + 8] = far[np.random.randint(len(far))]
    return np.exp2(a.ravel()).repeat(32)


def f64(x):
    return np.asarray(x).astype(np.float64)


def striped(idx):
    return np.tile(np.asarray(idx).reshape(-1, 16).T, (8, 1)).astype(np.uint16)


def unstriped(offs):
    return offs[:16].T.reshape(-1).astype(np.int64)


E2M1 = np.array([0.0, 0.5, 1.0, 1.5, 2.0, 3.0, 4.0, 6.0, -0.0, -0.5, -1.0, -1.5, -2.0, -3.0, -4.0, -6.0])


def pack_weight(w, fmt):
    k, n = w.shape
    w = f64(np.asarray(w, np.float32).astype(ml_dtypes.bfloat16)).reshape(k // 32, 32, n)
    amax = np.abs(w).max(1)
    if fmt == "e4m3":
        byte = np.frexp(amax)[1] - 1 + 127 - 7
    else:
        mant, ex = np.frexp(amax / 6.0)
        byte = np.where(mant > 0.5, ex, ex - 1) + 127
    byte = np.clip(np.where(amax > 0, byte, 1), 1, 254)
    scaled = (w * np.exp2(127.0 - byte)[:, None, :]).reshape(k, n).astype(np.float32)
    by_word = np.ascontiguousarray(scaled.reshape(k // 512, 128, 4, n).transpose(0, 1, 3, 2))
    if fmt == "e4m3":
        words = by_word.astype(ml_dtypes.float8_e4m3fn).view(np.uint8)
    else:
        c = by_word.astype(ml_dtypes.float4_e2m1fn).view(np.uint8) & 0xF
        words = (c[..., 0::2] | (c[..., 1::2] << 4)).reshape(k // 512, 128, 2 * n)
    return np.ascontiguousarray(words), np.ascontiguousarray(byte.astype(np.uint8).reshape(k // 512, 16, n))


def unpack_weight(words, scales, fmt):
    g, _, n = scales.shape
    words = np.ascontiguousarray(words).reshape(g, 128, n, -1)
    if fmt == "e4m3":
        vals = words.view(ml_dtypes.float8_e4m3fn).astype(np.float64)
    else:
        nib = np.empty((g, 128, n, 4), np.uint8)
        nib[..., 0::2] = words & 0xF
        nib[..., 1::2] = words >> 4
        vals = E2M1[nib]
    vals = vals * np.repeat(np.exp2(scales.astype(np.float64) - 127.0), 8, axis=1)[..., None]
    return vals.transpose(0, 1, 3, 2).reshape(g * 512, n)


B, N, T, D, DV, NQ = 2, 512, 2048, 1024, 0, 128
PAGE = 32


def setup_inputs():
    n = np.random.standard_normal
    pages = np.random.permutation(T // PAGE)[:B * N // PAGE]
    idx = (pages[:, None] * PAGE + np.arange(PAGE)[None, :]).reshape(-1)
    s = mx_kscale(D)[:, None]
    r = np.random.uniform(0.5, 2.0, T)
    kp = pack_weight(n((D, T)) / s / r, "e2m1")
    return {
        "qT": (n((B, D, NQ)) * s * (1.00 / np.sqrt(D))).astype(np.float32),
        "k_words": np.ascontiguousarray(kp[0].reshape(1, 2, 128, T, 2).transpose(0, 2, 3, 1, 4)).reshape(1, 128, T, 4),
        "k_scales": kp[1],
        "ts": np.tile(r, (128, 1)).astype(np.float32),
        "offs": striped(idx),
    }


def reference(qT, k_words, k_scales, ts, offs):
    idx = unstriped(offs)
    pool = unpack_weight(k_words.reshape(1, 128, T, 2, 2).transpose(0, 3, 1, 2, 4).reshape(2, 128, 2 * T), k_scales, "e2m1")
    pick = lambda x: x[:, idx].reshape(x.shape[0], B, N).transpose(1, 0, 2)
    a = mxq(f64(qT), 1, "e4m3").transpose(0, 2, 1) @ pick(pool)
    a = a * pick(f64(ts))[:, :1, :]
    out = np.zeros((B, NQ, T))
    for b in range(B):
        out[b][:, idx[b * N:(b + 1) * N]] = a[b]
    return out

@@ -1,0 +1,134 @@
+from contextlib import ExitStack
+
+import concourse.mybir as mybir
+from concourse.masks import make_identity
+
+B, N, T, D, NQ = 2, 512, 2048, 1024, 128
+P = 128
+PACK = 4
+K_PASS = P * PACK
+PASSES = D // K_PASS
+LIST_COLS = N // 16
+FLOPS = 2 * B * NQ * N * D
+
+F32 = mybir.dt.float32
+BF16 = mybir.dt.bfloat16
+I32 = mybir.dt.int32
+U32 = mybir.dt.uint32
+U16 = mybir.dt.uint16
+U8 = mybir.dt.uint8
+FP8X4 = mybir.dt.float8_e4m3fn_x4
+FP4X4 = mybir.dt.float4_e2m1fn_x4
+MULT = mybir.AluOpType.mult
+
+SCALE_ROW0 = 96
+TS_COLS = T // P
+
+
+def tile_attend_sddmm_ts_kernel(tc, qT, k_words, k_scales, ts, offs, out):
+    nc = tc.nc
+    with ExitStack() as ctx:
+        keep = ctx.enter_context(tc.tile_pool(name="keep", bufs=1))
+        psum = ctx.enter_context(tc.psum_pool(name="psum", bufs=1))
+
+        offsets = keep.tile([P, B * LIST_COLS], U16, name="offsets")
+        scale_pool = keep.tile([P, T], U8, name="scale_pool", align_bytes=64)
+        ts_cols = keep.tile([P, TS_COLS], F32, name="ts_cols")
+        word_pool = keep.tile([P, T], I32, name="word_pool", align_bytes=64)
+        q_raw = [[keep.tile([P, PACK, NQ], F32, name="q_raw_%d_%d" % (b, o)) for o in range(PASSES)] for b in range(B)]
+
+        nc.sync.dma_start(offsets[:], offs)
+        nc.sync.dma_start(out=scale_pool[SCALE_ROW0:P, :].bitcast(I32),
+                          in_=k_scales.rearrange("o f t -> f o t").bitcast(I32))
+        nc.sync.dma_start(out=ts_cols[:], in_=ts[0, :].rearrange("(p c) -> p c", c=TS_COLS))
+        nc.sync.dma_start(out=word_pool[:], in_=k_words[0].rearrange("p t x -> p (t x)").bitcast(I32))
+        for b in range(B):
+            for o in range(PASSES):
+                nc.sync.dma_start(out=q_raw[b][o][:],
+                                  in_=qT[b, o * K_PASS:(o + 1) * K_PASS, :].rearrange("(p j) q -> p j q", j=PACK))
+
+        def list_of(b):
+            return offsets[:, b * LIST_COLS:(b + 1) * LIST_COLS]
+
+        identity = keep.tile([P, P], F32, name="identity")
+        make_identity(nc, identity[:])
+
+        key_scales = keep.tile([P, PASSES, B * N], U8, name="key_scales", align_bytes=64)
+        rows = [keep.tile([P, T], F32, name="rows_%d" % b) for b in range(B)]
+        nc.vector.memset(scale_pool[0:SCALE_ROW0, :].bitcast(I32), 0)
+        nc.vector.memset(key_scales[:].rearrange("p o n -> p (o n)").bitcast(I32), 0)
+        for b in range(B):
+            nc.vector.memset(rows[b][:], 0.0)
+
+        picked_scales = keep.tile([P, B * N], U8, name="picked_scales", align_bytes=64)
+        nc.vector.tensor_copy(picked_scales[:], scale_pool[:].indirect(offsets[:]))
+        for quad in (0, 2, 1, 3):
+            src0 = SCALE_ROW0 + 8 * quad
+            nc.scalar.dma_start(out=key_scales[32 * quad:32 * quad + 4, :, :].bitcast(I32),
+                                in_=picked_scales[src0:src0 + 8, :].bitcast(I32))
+
+        ts_pool = keep.tile([P, T], F32, name="ts_pool")
+        ts_view = ts_pool[:].rearrange("p (n c) -> p n c", c=TS_COLS)
+        for j in range(TS_COLS // 4):
+            bank = psum.tile([P, 4, P], F32, name="ts_bank_%d" % j)
+            for c in range(4):
+                col = 4 * j + c
+                nc.tensor.transpose(bank[:, c, :], ts_cols[:, col:col + 1].to_broadcast([P, P]), identity[:])
+            nc.scalar.copy(out=ts_view[:, :, 4 * j:4 * j + 4], in_=bank[:].rearrange("p c n -> p n c"))
+
+        picked_words = [keep.tile([P, N], U32, name="picked_words_%d" % b, align_bytes=64) for b in range(B)]
+        key_words = [[keep.tile([P, 2 * N], U8, name="key_words_%d_%d" % (b, o), align_bytes=64)
+                      for o in range(PASSES)] for b in range(B)]
+        q_bf = [[keep.tile([P, NQ, PACK], BF16, name="q_bf_%d_%d" % (b, o), align_bytes=64)
+                 for o in range(PASSES)] for b in range(B)]
+        q_codes = [[keep.tile([P, NQ], U32, name="q_codes_%d_%d" % (b, o), align_bytes=64)
+                    for o in range(PASSES)] for b in range(B)]
+        q_scales = [[keep.tile([P, NQ], U8, name="q_scales_%d_%d" % (b, o), align_bytes=64)
+                     for o in range(PASSES)] for b in range(B)]
+        picked_ts = [keep.tile([P, N], F32, name="picked_ts_%d" % b) for b in range(B)]
+        scores = [keep.tile([P, N], F32, name="scores_%d" % b) for b in range(B)]
+        acc = [psum.tile([NQ, N], F32, name="acc_%d" % b) for b in range(B)]
+
+        def gather_keys(b):
+            nc.vector.tensor_copy(picked_words[b][:], word_pool[:].bitcast(U32).indirect(list_of(b)))
+            halves = picked_words[b][:].bitcast(U16).rearrange("p (n o) -> p o n", o=PASSES)
+            for o in range(PASSES):
+                nc.vector.tensor_copy(key_words[b][o][:].bitcast(U16), halves[:, o, :])
+
+        def round_queries(b):
+            for o in range(PASSES):
+                nc.scalar.copy(out=q_bf[b][o][:].rearrange("p (c i) j -> p c j i", i=4),
+                               in_=q_raw[b][o][:].rearrange("p j (c i) -> p c j i", i=4))
+
+        def quantise_queries(b):
+            for o in range(PASSES):
+                nc.vector.quantize_mx(out=q_codes[b][o][:].bitcast(FP8X4), scales=q_scales[b][o][:],
+                                      in_=q_bf[b][o][:].rearrange("p q j -> p (q j)"))
+
+        def score(b):
+            for o in range(PASSES):
+                nc.tensor.matmul_mx(out=acc[b][:], lhsT=q_codes[b][o][:].bitcast(FP8X4), lhsT_scale=q_scales[b][o][:],
+                                    rhs=key_words[b][o][:].bitcast(FP4X4),
+                                    rhs_scale=key_scales[:, o, b * N:(b + 1) * N],
+                                    start=(o == 0), stop=(o == PASSES - 1))
+            nc.scalar.copy(out=scores[b][:], in_=acc[b][:])
+
+        def gather_ts(b):
+            nc.vector.tensor_copy(picked_ts[b][:], ts_pool[:].indirect(list_of(b)))
+
+        def place(b):
+            nc.vector.tensor_tensor(rows[b][:].indirect(list_of(b)), scores[b][:], picked_ts[b][:], MULT)
+            nc.sync.dma_start(out=out[b], in_=rows[b][:])
+
+        gather_keys(0)
+        round_queries(0)
+        quantise_queries(0)
+        score(0)
+        gather_keys(1)
+        gather_ts(0)
+        round_queries(1)
+        quantise_queries(1)
+        score(1)
+        place(0)
+        gather_ts(1)
+        place(1)

@@ -32,20 +32,24 @@ def tile_attend_sddmm_ts_kernel(tc, qT, k_words, k_scales, ts, offs, out):
         psum = ctx.enter_context(tc.psum_pool(name="psum", bufs=1))
 
         offsets = keep.tile([P, B * LIST_COLS], U16, name="offsets")
-        scale_pool = keep.tile([P, T], U8, name="scale_pool", align_bytes=64)
-        ts_cols = keep.tile([P, TS_COLS], F32, name="ts_cols")
+        scale_pool = keep.tile([P, T], U8, name="scale_pool", tag="scales_then_q", align_bytes=64)
+        ts_cols = [keep.tile([P, TS_COLS // 2], F32, name="ts_cols_%d" % h) for h in range(2)]
         word_pool = keep.tile([P, T], I32, name="word_pool", align_bytes=64)
-        q_raw = [[keep.tile([P, PACK, NQ], F32, name="q_raw_%d_%d" % (b, o)) for o in range(PASSES)] for b in range(B)]
+        q_first = keep.tile([P, PASSES, PACK, NQ], F32, name="q_first")
+        ts_row = ts[0, :].rearrange("(p c) -> p c", c=TS_COLS)
+
+        def load_queries(b, dst):
+            for o in range(PASSES):
+                nc.sync.dma_start(out=dst[:, o, :, :],
+                                  in_=qT[b, o * K_PASS:(o + 1) * K_PASS, :].rearrange("(p j) q -> p j q", j=PACK))
 
         nc.sync.dma_start(offsets[:], offs)
         nc.sync.dma_start(out=scale_pool[SCALE_ROW0:P, :].bitcast(I32),
                           in_=k_scales.rearrange("o f t -> f o t").bitcast(I32))
-        nc.sync.dma_start(out=ts_cols[:], in_=ts[0, :].rearrange("(p c) -> p c", c=TS_COLS))
+        nc.sync.dma_start(out=ts_cols[0][:], in_=ts_row[:, 0:TS_COLS // 2])
         nc.sync.dma_start(out=word_pool[:], in_=k_words[0].rearrange("p t x -> p (t x)").bitcast(I32))
-        for b in range(B):
-            for o in range(PASSES):
-                nc.sync.dma_start(out=q_raw[b][o][:],
-                                  in_=qT[b, o * K_PASS:(o + 1) * K_PASS, :].rearrange("(p j) q -> p j q", j=PACK))
+        load_queries(0, q_first)
+        nc.sync.dma_start(out=ts_cols[1][:], in_=ts_row[:, TS_COLS // 2:TS_COLS])
 
         def list_of(b):
             return offsets[:, b * LIST_COLS:(b + 1) * LIST_COLS]
@@ -56,7 +60,6 @@ def tile_attend_sddmm_ts_kernel(tc, qT, k_words, k_scales, ts, offs, out):
         key_scales = keep.tile([P, PASSES, B * N], U8, name="key_scales", align_bytes=64)
         rows = [keep.tile([P, T], F32, name="rows_%d" % b) for b in range(B)]
         nc.vector.memset(scale_pool[0:SCALE_ROW0, :].bitcast(I32), 0)
-        nc.vector.memset(key_scales[:].rearrange("p o n -> p (o n)").bitcast(I32), 0)
         for b in range(B):
             nc.vector.memset(rows[b][:], 0.0)
 
@@ -64,17 +67,23 @@ def tile_attend_sddmm_ts_kernel(tc, qT, k_words, k_scales, ts, offs, out):
         nc.vector.tensor_copy(picked_scales[:], scale_pool[:].indirect(offsets[:]))
         for quad in (0, 2, 1, 3):
             src0 = SCALE_ROW0 + 8 * quad
-            nc.scalar.dma_start(out=key_scales[32 * quad:32 * quad + 4, :, :].bitcast(I32),
-                                in_=picked_scales[src0:src0 + 8, :].bitcast(I32))
+            nc.sync.dma_start(out=key_scales[32 * quad:32 * quad + 4, :, :].bitcast(I32),
+                              in_=picked_scales[src0:src0 + 8, :].bitcast(I32))
+        q_second = keep.tile([P, PASSES, PACK, NQ], F32, name="q_second", tag="scales_then_q", align_bytes=64)
+        load_queries(1, q_second)
+        q_raw = [q_first, q_second]
 
         ts_pool = keep.tile([P, T], F32, name="ts_pool")
         ts_view = ts_pool[:].rearrange("p (n c) -> p n c", c=TS_COLS)
-        for j in range(TS_COLS // 4):
-            bank = psum.tile([P, 4, P], F32, name="ts_bank_%d" % j)
-            for c in range(4):
-                col = 4 * j + c
-                nc.tensor.transpose(bank[:, c, :], ts_cols[:, col:col + 1].to_broadcast([P, P]), identity[:])
-            nc.scalar.copy(out=ts_view[:, :, 4 * j:4 * j + 4], in_=bank[:].rearrange("p c n -> p n c"))
+
+        def spread_ts(h):
+            for j in range(2):
+                bank = psum.tile([P, 4, P], F32, name="ts_bank_%d_%d" % (h, j))
+                for c in range(4):
+                    col = 4 * j + c
+                    nc.tensor.transpose(bank[:, c, :], ts_cols[h][:, col:col + 1].to_broadcast([P, P]), identity[:])
+                first = 8 * h + 4 * j
+                nc.scalar.copy(out=ts_view[:, :, first:first + 4], in_=bank[:].rearrange("p c n -> p n c"))
 
         picked_words = [keep.tile([P, N], U32, name="picked_words_%d" % b, align_bytes=64) for b in range(B)]
         key_words = [[keep.tile([P, 2 * N], U8, name="key_words_%d_%d" % (b, o), align_bytes=64)
@@ -98,7 +107,7 @@ def tile_attend_sddmm_ts_kernel(tc, qT, k_words, k_scales, ts, offs, out):
         def round_queries(b):
             for o in range(PASSES):
                 nc.scalar.copy(out=q_bf[b][o][:].rearrange("p (c i) j -> p c j i", i=4),
-                               in_=q_raw[b][o][:].rearrange("p j (c i) -> p c j i", i=4))
+                               in_=q_raw[b][:, o, :, :].rearrange("p j (c i) -> p c j i", i=4))
 
         def quantise_queries(b):
             for o in range(PASSES):
@@ -120,9 +129,11 @@ def tile_attend_sddmm_ts_kernel(tc, qT, k_words, k_scales, ts, offs, out):
             nc.vector.tensor_tensor(rows[b][:].indirect(list_of(b)), scores[b][:], picked_ts[b][:], MULT)
             nc.sync.dma_start(out=out[b], in_=rows[b][:])
 
+        spread_ts(0)
         gather_keys(0)
         round_queries(0)
         quantise_queries(0)
+        spread_ts(1)
         score(0)
         gather_keys(1)
         gather_ts(0)

@@ -23,6 +23,8 @@ MULT = mybir.AluOpType.mult
 
 SCALE_ROW0 = 96
 TS_COLS = T // P
+TS_PARTS = ((0, 12), (12, 16))
+HALF = N // 2
 
 
 def tile_attend_sddmm_ts_kernel(tc, qT, k_words, k_scales, ts, offs, out):
@@ -33,23 +35,23 @@ def tile_attend_sddmm_ts_kernel(tc, qT, k_words, k_scales, ts, offs, out):
 
         offsets = keep.tile([P, B * LIST_COLS], U16, name="offsets")
         scale_pool = keep.tile([P, T], U8, name="scale_pool", tag="scales_then_q", align_bytes=64)
-        ts_cols = [keep.tile([P, TS_COLS // 2], F32, name="ts_cols_%d" % h) for h in range(2)]
+        ts_cols = [keep.tile([P, c1 - c0], F32, name="ts_cols_%d" % c0) for c0, c1 in TS_PARTS]
         word_pool = keep.tile([P, T], I32, name="word_pool", align_bytes=64)
         q_first = keep.tile([P, PASSES, PACK, NQ], F32, name="q_first")
         ts_row = ts[0, :].rearrange("(p c) -> p c", c=TS_COLS)
 
-        def load_queries(b, dst):
-            for o in range(PASSES):
-                nc.sync.dma_start(out=dst[:, o, :, :],
-                                  in_=qT[b, o * K_PASS:(o + 1) * K_PASS, :].rearrange("(p j) q -> p j q", j=PACK))
+        def load_queries(b, o, dst):
+            nc.sync.dma_start(out=dst[:, o, :, :],
+                              in_=qT[b, o * K_PASS:(o + 1) * K_PASS, :].rearrange("(p j) q -> p j q", j=PACK))
 
         nc.sync.dma_start(offsets[:], offs)
         nc.sync.dma_start(out=scale_pool[SCALE_ROW0:P, :].bitcast(I32),
                           in_=k_scales.rearrange("o f t -> f o t").bitcast(I32))
-        nc.sync.dma_start(out=ts_cols[0][:], in_=ts_row[:, 0:TS_COLS // 2])
+        nc.sync.dma_start(out=ts_cols[0][:], in_=ts_row[:, TS_PARTS[0][0]:TS_PARTS[0][1]])
         nc.sync.dma_start(out=word_pool[:], in_=k_words[0].rearrange("p t x -> p (t x)").bitcast(I32))
-        load_queries(0, q_first)
-        nc.sync.dma_start(out=ts_cols[1][:], in_=ts_row[:, TS_COLS // 2:TS_COLS])
+        for o in range(PASSES):
+            load_queries(0, o, q_first)
+        nc.sync.dma_start(out=ts_cols[1][:], in_=ts_row[:, TS_PARTS[1][0]:TS_PARTS[1][1]])
 
         def list_of(b):
             return offsets[:, b * LIST_COLS:(b + 1) * LIST_COLS]
@@ -61,7 +63,7 @@ def tile_attend_sddmm_ts_kernel(tc, qT, k_words, k_scales, ts, offs, out):
         rows = [keep.tile([P, T], F32, name="rows_%d" % b) for b in range(B)]
         nc.vector.memset(scale_pool[0:SCALE_ROW0, :].bitcast(I32), 0)
         for b in range(B):
-            nc.vector.memset(rows[b][:], 0.0)
+            nc.vector.memset(rows[b][:].bitcast(I32), 0)
 
         picked_scales = keep.tile([P, B * N], U8, name="picked_scales", align_bytes=64)
         nc.vector.tensor_copy(picked_scales[:], scale_pool[:].indirect(offsets[:]))
@@ -70,19 +72,19 @@ def tile_attend_sddmm_ts_kernel(tc, qT, k_words, k_scales, ts, offs, out):
             nc.sync.dma_start(out=key_scales[32 * quad:32 * quad + 4, :, :].bitcast(I32),
                               in_=picked_scales[src0:src0 + 8, :].bitcast(I32))
         q_second = keep.tile([P, PASSES, PACK, NQ], F32, name="q_second", tag="scales_then_q", align_bytes=64)
-        load_queries(1, q_second)
+        for o in range(PASSES):
+            load_queries(1, o, q_second)
         q_raw = [q_first, q_second]
 
         ts_pool = keep.tile([P, T], F32, name="ts_pool")
         ts_view = ts_pool[:].rearrange("p (n c) -> p n c", c=TS_COLS)
 
         def spread_ts(h):
-            for j in range(2):
-                bank = psum.tile([P, 4, P], F32, name="ts_bank_%d_%d" % (h, j))
+            for first in range(TS_PARTS[h][0], TS_PARTS[h][1], 4):
+                bank = psum.tile([P, 4, P], F32, name="ts_bank_%d" % first)
                 for c in range(4):
-                    col = 4 * j + c
+                    col = first + c - TS_PARTS[h][0]
                     nc.tensor.transpose(bank[:, c, :], ts_cols[h][:, col:col + 1].to_broadcast([P, P]), identity[:])
-                first = 8 * h + 4 * j
                 nc.scalar.copy(out=ts_view[:, :, first:first + 4], in_=bank[:].rearrange("p c n -> p n c"))
 
         picked_words = [keep.tile([P, N], U32, name="picked_words_%d" % b, align_bytes=64) for b in range(B)]
@@ -94,8 +96,6 @@ def tile_attend_sddmm_ts_kernel(tc, qT, k_words, k_scales, ts, offs, out):
                     for o in range(PASSES)] for b in range(B)]
         q_scales = [[keep.tile([P, NQ], U8, name="q_scales_%d_%d" % (b, o), align_bytes=64)
                      for o in range(PASSES)] for b in range(B)]
-        picked_ts = [keep.tile([P, N], F32, name="picked_ts_%d" % b) for b in range(B)]
-        scores = [keep.tile([P, N], F32, name="scores_%d" % b) for b in range(B)]
         acc = [psum.tile([NQ, N], F32, name="acc_%d" % b) for b in range(B)]
 
         def gather_keys(b):
@@ -120,13 +120,24 @@ def tile_attend_sddmm_ts_kernel(tc, qT, k_words, k_scales, ts, offs, out):
                                     rhs=key_words[b][o][:].bitcast(FP4X4),
                                     rhs_scale=key_scales[:, o, b * N:(b + 1) * N],
                                     start=(o == 0), stop=(o == PASSES - 1))
-            nc.scalar.copy(out=scores[b][:], in_=acc[b][:])
+
+        def read_scores(b, tag):
+            scores = keep.tile([P, N], F32, name="scores_%d" % b, tag=tag, align_bytes=64)
+            for h in range(2):
+                nc.scalar.copy(out=scores[:, h * HALF:(h + 1) * HALF], in_=acc[b][:, h * HALF:(h + 1) * HALF])
+            return scores
 
         def gather_ts(b):
-            nc.vector.tensor_copy(picked_ts[b][:], ts_pool[:].indirect(list_of(b)))
+            picked_ts = keep.tile([P, N], F32, name="picked_ts")
+            nc.vector.tensor_copy(picked_ts[:], ts_pool[:].indirect(list_of(b)))
+            return picked_ts
 
-        def place(b):
-            nc.vector.tensor_tensor(rows[b][:].indirect(list_of(b)), scores[b][:], picked_ts[b][:], MULT)
+        def place(b, scores, picked_ts):
+            for h in range(2):
+                col0 = b * LIST_COLS + h * LIST_COLS // 2
+                slots = slice(h * HALF, (h + 1) * HALF)
+                nc.vector.tensor_tensor(rows[b][:].indirect(offsets[:, col0:col0 + LIST_COLS // 2]),
+                                        scores[:, slots], picked_ts[:, slots], MULT)
             nc.sync.dma_start(out=out[b], in_=rows[b][:])
 
         spread_ts(0)
@@ -136,10 +147,9 @@ def tile_attend_sddmm_ts_kernel(tc, qT, k_words, k_scales, ts, offs, out):
         spread_ts(1)
         score(0)
         gather_keys(1)
-        gather_ts(0)
+        ts_first = gather_ts(0)
         round_queries(1)
         quantise_queries(1)
         score(1)
-        place(0)
-        gather_ts(1)
-        place(1)
+        place(0, read_scores(0, "scales_then_q"), ts_first)
+        place(1, read_scores(1, "scores_second"), gather_ts(1))

@@ -23,8 +23,7 @@ MULT = mybir.AluOpType.mult
 
 SCALE_ROW0 = 96
 TS_COLS = T // P
-TS_PARTS = ((0, 12), (12, 16))
-HALF = N // 2
+BANK_BLOCKS = 4
 
 
 def tile_attend_sddmm_ts_kernel(tc, qT, k_words, k_scales, ts, offs, out):
@@ -33,123 +32,110 @@ def tile_attend_sddmm_ts_kernel(tc, qT, k_words, k_scales, ts, offs, out):
         keep = ctx.enter_context(tc.tile_pool(name="keep", bufs=1))
         psum = ctx.enter_context(tc.psum_pool(name="psum", bufs=1))
 
-        offsets = keep.tile([P, B * LIST_COLS], U16, name="offsets")
-        scale_pool = keep.tile([P, T], U8, name="scale_pool", tag="scales_then_q", align_bytes=64)
-        ts_cols = [keep.tile([P, c1 - c0], F32, name="ts_cols_%d" % c0) for c0, c1 in TS_PARTS]
-        word_pool = keep.tile([P, T], I32, name="word_pool", align_bytes=64)
-        q_first = keep.tile([P, PASSES, PACK, NQ], F32, name="q_first")
-        ts_row = ts[0, :].rearrange("(p c) -> p c", c=TS_COLS)
+        def sbuf(shape, dtype, name, tag=None):
+            return keep.tile(shape, dtype, name=name, tag=tag or name, align_bytes=64)
 
-        def load_queries(b, o, dst):
-            nc.sync.dma_start(out=dst[:, o, :, :],
+        def load_queries(b, o, tag=None):
+            raw = sbuf([P, PACK, NQ], F32, "q_raw_%d_%d" % (b, o), tag)
+            nc.sync.dma_start(out=raw[:],
                               in_=qT[b, o * K_PASS:(o + 1) * K_PASS, :].rearrange("(p j) q -> p j q", j=PACK))
+            return raw
 
+        offsets = keep.tile([P, B * LIST_COLS], U16, name="offsets")
+        ts_cols = sbuf([P, TS_COLS], F32, "ts_cols")
+        scale_pool = sbuf([P, T], U8, "scale_pool", "slot_a")
+        word_pool = sbuf([P, T], I32, "word_pool")
+        nc.sync.dma_start(out=ts_cols[:], in_=ts[0, :].rearrange("(p c) -> p c", c=TS_COLS))
         nc.sync.dma_start(offsets[:], offs)
         nc.sync.dma_start(out=scale_pool[SCALE_ROW0:P, :].bitcast(I32),
                           in_=k_scales.rearrange("o f t -> f o t").bitcast(I32))
-        nc.sync.dma_start(out=ts_cols[0][:], in_=ts_row[:, TS_PARTS[0][0]:TS_PARTS[0][1]])
         nc.sync.dma_start(out=word_pool[:], in_=k_words[0].rearrange("p t x -> p (t x)").bitcast(I32))
-        for o in range(PASSES):
-            load_queries(0, o, q_first)
-        nc.sync.dma_start(out=ts_cols[1][:], in_=ts_row[:, TS_PARTS[1][0]:TS_PARTS[1][1]])
+        q_raw = {(0, 0): load_queries(0, 0), (0, 1): load_queries(0, 1, "slot_b"), (1, 0): load_queries(1, 0)}
 
         def list_of(b):
             return offsets[:, b * LIST_COLS:(b + 1) * LIST_COLS]
 
-        identity = keep.tile([P, P], F32, name="identity")
+        identity = sbuf([P, P], F32, "identity")
         make_identity(nc, identity[:])
 
-        key_scales = keep.tile([P, PASSES, B * N], U8, name="key_scales", align_bytes=64)
-        rows = [keep.tile([P, T], F32, name="rows_%d" % b) for b in range(B)]
+        rows = [sbuf([P, T], F32, "rows_%d" % b) for b in range(B)]
         nc.vector.memset(scale_pool[0:SCALE_ROW0, :].bitcast(I32), 0)
         for b in range(B):
             nc.vector.memset(rows[b][:].bitcast(I32), 0)
 
-        picked_scales = keep.tile([P, B * N], U8, name="picked_scales", align_bytes=64)
+        picked_scales = sbuf([P, B * N], U8, "picked_scales")
+        key_scales = sbuf([P, PASSES, B * N], U8, "key_scales")
         nc.vector.tensor_copy(picked_scales[:], scale_pool[:].indirect(offsets[:]))
         for quad in (0, 2, 1, 3):
             src0 = SCALE_ROW0 + 8 * quad
             nc.sync.dma_start(out=key_scales[32 * quad:32 * quad + 4, :, :].bitcast(I32),
                               in_=picked_scales[src0:src0 + 8, :].bitcast(I32))
-        q_second = keep.tile([P, PASSES, PACK, NQ], F32, name="q_second", tag="scales_then_q", align_bytes=64)
-        for o in range(PASSES):
-            load_queries(1, o, q_second)
-        q_raw = [q_first, q_second]
+        q_raw[1, 1] = load_queries(1, 1, "slot_a")
 
-        ts_pool = keep.tile([P, T], F32, name="ts_pool")
+        ts_pool = sbuf([P, T], F32, "ts_pool")
         ts_view = ts_pool[:].rearrange("p (n c) -> p n c", c=TS_COLS)
+        for first in range(0, TS_COLS, BANK_BLOCKS):
+            bank = psum.tile([P, BANK_BLOCKS, P], F32, name="ts_bank_%d" % first)
+            for c in range(BANK_BLOCKS):
+                col = first + c
+                nc.tensor.transpose(bank[:, c, :], ts_cols[:, col:col + 1].to_broadcast([P, P]), identity[:])
+            nc.scalar.copy(out=ts_view[:, :, first:first + BANK_BLOCKS], in_=bank[:].rearrange("p c n -> p n c"))
 
-        def spread_ts(h):
-            for first in range(TS_PARTS[h][0], TS_PARTS[h][1], 4):
-                bank = psum.tile([P, 4, P], F32, name="ts_bank_%d" % first)
-                for c in range(4):
-                    col = first + c - TS_PARTS[h][0]
-                    nc.tensor.transpose(bank[:, c, :], ts_cols[h][:, col:col + 1].to_broadcast([P, P]), identity[:])
-                nc.scalar.copy(out=ts_view[:, :, first:first + 4], in_=bank[:].rearrange("p c n -> p n c"))
+        def gather_words(b):
+            picked = sbuf([P, N], U32, "picked_words_%d" % b)
+            nc.vector.tensor_copy(picked[:], word_pool[:].bitcast(U32).indirect(list_of(b)))
+            return picked
 
-        picked_words = [keep.tile([P, N], U32, name="picked_words_%d" % b, align_bytes=64) for b in range(B)]
-        key_words = [[keep.tile([P, 2 * N], U8, name="key_words_%d_%d" % (b, o), align_bytes=64)
-                      for o in range(PASSES)] for b in range(B)]
-        q_bf = [[keep.tile([P, NQ, PACK], BF16, name="q_bf_%d_%d" % (b, o), align_bytes=64)
-                 for o in range(PASSES)] for b in range(B)]
-        q_codes = [[keep.tile([P, NQ], U32, name="q_codes_%d_%d" % (b, o), align_bytes=64)
-                    for o in range(PASSES)] for b in range(B)]
-        q_scales = [[keep.tile([P, NQ], U8, name="q_scales_%d_%d" % (b, o), align_bytes=64)
-                     for o in range(PASSES)] for b in range(B)]
-        acc = [psum.tile([NQ, N], F32, name="acc_%d" % b) for b in range(B)]
+        def part_words(b, picked, tag=None):
+            keys = sbuf([P, PASSES, 2 * N], U8, "key_words_%d" % b, tag)
+            nc.vector.tensor_copy(keys[:].bitcast(U16),
+                                  picked[:].bitcast(U16).rearrange("p (n o) -> p o n", o=PASSES))
+            return keys
 
-        def gather_keys(b):
-            nc.vector.tensor_copy(picked_words[b][:], word_pool[:].bitcast(U32).indirect(list_of(b)))
-            halves = picked_words[b][:].bitcast(U16).rearrange("p (n o) -> p o n", o=PASSES)
+        def round_queries(b, o, rounded):
+            nc.scalar.copy(out=rounded.rearrange("p (c i) j -> p c j i", i=4),
+                           in_=q_raw[b, o][:].rearrange("p j (c i) -> p c j i", i=4))
+
+        def quantise(rounded, codes, scales):
+            nc.vector.quantize_mx(out=codes.bitcast(FP8X4), scales=scales, in_=rounded)
+
+        q_codes = [sbuf([P, PASSES, NQ], U32, "q_codes_%d" % b) for b in range(B)]
+        q_scales = [sbuf([P, PASSES, NQ], U8, "q_scales_%d" % b) for b in range(B)]
+
+        def score(b, keys, tag=None):
+            acc = psum.tile([NQ, N], F32, name="acc_%d" % b)
             for o in range(PASSES):
-                nc.vector.tensor_copy(key_words[b][o][:].bitcast(U16), halves[:, o, :])
-
-        def round_queries(b):
-            for o in range(PASSES):
-                nc.scalar.copy(out=q_bf[b][o][:].rearrange("p (c i) j -> p c j i", i=4),
-                               in_=q_raw[b][:, o, :, :].rearrange("p j (c i) -> p c j i", i=4))
-
-        def quantise_queries(b):
-            for o in range(PASSES):
-                nc.vector.quantize_mx(out=q_codes[b][o][:].bitcast(FP8X4), scales=q_scales[b][o][:],
-                                      in_=q_bf[b][o][:].rearrange("p q j -> p (q j)"))
-
-        def score(b):
-            for o in range(PASSES):
-                nc.tensor.matmul_mx(out=acc[b][:], lhsT=q_codes[b][o][:].bitcast(FP8X4), lhsT_scale=q_scales[b][o][:],
-                                    rhs=key_words[b][o][:].bitcast(FP4X4),
+                nc.tensor.matmul_mx(out=acc[:], lhsT=q_codes[b][:, o, :].bitcast(FP8X4), lhsT_scale=q_scales[b][:, o, :],
+                                    rhs=keys[:, o, :].bitcast(FP4X4),
                                     rhs_scale=key_scales[:, o, b * N:(b + 1) * N],
                                     start=(o == 0), stop=(o == PASSES - 1))
-
-        def read_scores(b, tag):
-            scores = keep.tile([P, N], F32, name="scores_%d" % b, tag=tag, align_bytes=64)
-            for h in range(2):
-                nc.scalar.copy(out=scores[:, h * HALF:(h + 1) * HALF], in_=acc[b][:, h * HALF:(h + 1) * HALF])
+            scores = sbuf([P, N], F32, "scores_%d" % b, tag)
+            nc.scalar.copy(out=scores[:], in_=acc[:])
             return scores
 
         def gather_ts(b):
-            picked_ts = keep.tile([P, N], F32, name="picked_ts")
+            picked_ts = sbuf([P, N], F32, "picked_ts_%d" % b, "slot_b")
             nc.vector.tensor_copy(picked_ts[:], ts_pool[:].indirect(list_of(b)))
             return picked_ts
 
         def place(b, scores, picked_ts):
-            for h in range(2):
-                col0 = b * LIST_COLS + h * LIST_COLS // 2
-                slots = slice(h * HALF, (h + 1) * HALF)
-                nc.vector.tensor_tensor(rows[b][:].indirect(offsets[:, col0:col0 + LIST_COLS // 2]),
-                                        scores[:, slots], picked_ts[:, slots], MULT)
+            nc.vector.tensor_tensor(rows[b][:].indirect(list_of(b)), scores[:], picked_ts[:], MULT)
             nc.sync.dma_start(out=out[b], in_=rows[b][:])
 
-        spread_ts(0)
-        gather_keys(0)
-        round_queries(0)
-        quantise_queries(0)
-        spread_ts(1)
-        score(0)
-        gather_keys(1)
+        picked_words = [gather_words(b) for b in range(B)]
+        keys_first = part_words(0, picked_words[0])
+        for o in range(PASSES):
+            rounded = sbuf([P, NQ, PACK], BF16, "q_bf_0_%d" % o, "slot_c" if o == PASSES - 1 else None)
+            round_queries(0, o, rounded[:])
+            quantise(rounded[:].rearrange("p q j -> p (q j)"), q_codes[0][:, o, :], q_scales[0][:, o, :])
         ts_first = gather_ts(0)
-        round_queries(1)
-        quantise_queries(1)
-        score(1)
-        place(0, read_scores(0, "scales_then_q"), ts_first)
-        place(1, read_scores(1, "scores_second"), gather_ts(1))
+        keys_second = part_words(1, picked_words[1], "slot_c")
+        rounded = sbuf([P, PASSES, NQ, PACK], BF16, "q_bf_1")
+        for o in range(PASSES):
+            round_queries(1, o, rounded[:, o, :, :])
+        quantise(rounded[:].rearrange("p o q j -> p (o q j)"), q_codes[1][:].rearrange("p o q -> p (o q)"),
+                 q_scales[1][:].rearrange("p o q -> p (o q)"))
+        scores_first = score(0, keys_first, "slot_a")
+        scores_second = score(1, keys_second)
+        place(0, scores_first, ts_first)
+        place(1, scores_second, gather_ts(1))

@@ -1,7 +1,6 @@
 from contextlib import ExitStack
 
 import concourse.mybir as mybir
-from concourse.masks import make_identity
 
 B, N, T, D, NQ = 2, 512, 2048, 1024, 128
 P = 128
@@ -55,13 +54,16 @@ def tile_attend_sddmm_ts_kernel(tc, qT, k_words, k_scales, ts, offs, out):
         def list_of(b):
             return offsets[:, b * LIST_COLS:(b + 1) * LIST_COLS]
 
+        zeros = sbuf([P, P], F32, "zeros", "slot_d")
         identity = sbuf([P, P], F32, "identity")
-        make_identity(nc, identity[:])
-
-        rows = [sbuf([P, T], F32, "rows_%d" % b) for b in range(B)]
+        rows = [sbuf([P, T], F32, "rows_0")]
         nc.vector.memset(scale_pool[0:SCALE_ROW0, :].bitcast(I32), 0)
-        for b in range(B):
-            nc.vector.memset(rows[b][:].bitcast(I32), 0)
+        nc.vector.memset(rows[0][:].bitcast(I32), 0)
+        nc.vector.memset(zeros[:], 0.0)
+        nc.gpsimd.affine_select(out=identity[:], in_=zeros[:], compare_op=mybir.AluOpType.not_equal, fill=1.0,
+                                base=0, pattern=[[-1, P]], channel_multiplier=1)
+        rows.append(sbuf([P, T], F32, "rows_1", "slot_d"))
+        nc.gpsimd.memset(rows[1][:].bitcast(I32), 0)
 
         picked_scales = sbuf([P, B * N], U8, "picked_scales")
         key_scales = sbuf([P, PASSES, B * N], U8, "key_scales")

@@ -23,25 +23,29 @@ MULT = mybir.AluOpType.mult
 SCALE_ROW0 = 96
 TS_COLS = T // P
 BANK_BLOCKS = 4
+KIB = 1024
 
 
 def tile_attend_sddmm_ts_kernel(tc, qT, k_words, k_scales, ts, offs, out):
     nc = tc.nc
     with ExitStack() as ctx:
         keep = ctx.enter_context(tc.tile_pool(name="keep", bufs=1))
+        reused = ctx.enter_context(tc.tile_pool(name="reused", bufs=1))
         psum = ctx.enter_context(tc.psum_pool(name="psum", bufs=1))
 
-        def sbuf(shape, dtype, name, tag=None):
+        def sbuf(shape, dtype, name, tag=None, offset=None):
+            if offset is not None:
+                return reused.tile(shape, dtype, name=name, align_bytes=64, offset=offset)
             return keep.tile(shape, dtype, name=name, tag=tag or name, align_bytes=64)
 
-        def load_queries(b, o, tag=None):
-            raw = sbuf([P, PACK, NQ], F32, "q_raw_%d_%d" % (b, o), tag)
+        def load_queries(b, o, tag=None, offset=None):
+            raw = sbuf([P, PACK, NQ], F32, "q_raw_%d_%d" % (b, o), tag, offset)
             nc.sync.dma_start(out=raw[:],
                               in_=qT[b, o * K_PASS:(o + 1) * K_PASS, :].rearrange("(p j) q -> p j q", j=PACK))
             return raw
 
         offsets = keep.tile([P, B * LIST_COLS], U16, name="offsets")
-        ts_cols = sbuf([P, TS_COLS], F32, "ts_cols")
+        ts_cols = reused.tile([P, TS_COLS], F32, name="ts_cols", offset=KIB - 32)
         scale_pool = sbuf([P, T], U8, "scale_pool", "slot_a")
         word_pool = sbuf([P, T], I32, "word_pool")
         nc.sync.dma_start(out=ts_cols[:], in_=ts[0, :].rearrange("(p c) -> p c", c=TS_COLS))
@@ -49,7 +53,7 @@ def tile_attend_sddmm_ts_kernel(tc, qT, k_words, k_scales, ts, offs, out):
         nc.sync.dma_start(out=scale_pool[SCALE_ROW0:P, :].bitcast(I32),
                           in_=k_scales.rearrange("o f t -> f o t").bitcast(I32))
         nc.sync.dma_start(out=word_pool[:], in_=k_words[0].rearrange("p t x -> p (t x)").bitcast(I32))
-        q_raw = {(0, 0): load_queries(0, 0), (0, 1): load_queries(0, 1, "slot_b"), (1, 0): load_queries(1, 0)}
+        q_raw = {(0, 0): load_queries(0, 0), (0, 1): load_queries(0, 1, offset=3 * KIB), (1, 0): load_queries(1, 0)}
 
         def list_of(b):
             return offsets[:, b * LIST_COLS:(b + 1) * LIST_COLS]
@@ -57,9 +61,9 @@ def tile_attend_sddmm_ts_kernel(tc, qT, k_words, k_scales, ts, offs, out):
         zeros = sbuf([P, P], F32, "zeros", "slot_d")
         identity = sbuf([P, P], F32, "identity")
         rows = [sbuf([P, T], F32, "rows_0")]
+        nc.vector.memset(zeros[:], 0.0)
         nc.vector.memset(scale_pool[0:SCALE_ROW0, :].bitcast(I32), 0)
         nc.vector.memset(rows[0][:].bitcast(I32), 0)
-        nc.vector.memset(zeros[:], 0.0)
         nc.gpsimd.affine_select(out=identity[:], in_=zeros[:], compare_op=mybir.AluOpType.not_equal, fill=1.0,
                                 base=0, pattern=[[-1, P]], channel_multiplier=1)
         rows.append(sbuf([P, T], F32, "rows_1", "slot_d"))
@@ -76,33 +80,42 @@ def tile_attend_sddmm_ts_kernel(tc, qT, k_words, k_scales, ts, offs, out):
 
         ts_pool = sbuf([P, T], F32, "ts_pool")
         ts_view = ts_pool[:].rearrange("p (n c) -> p n c", c=TS_COLS)
-        for first in range(0, TS_COLS, BANK_BLOCKS):
-            bank = psum.tile([P, BANK_BLOCKS, P], F32, name="ts_bank_%d" % first)
+        banks = [psum.tile([P, BANK_BLOCKS, P], F32, name="ts_bank_%d" % k) for k in range(TS_COLS // BANK_BLOCKS)]
+
+        def empty_bank(k):
+            nc.scalar.copy(out=ts_view[:, :, k * BANK_BLOCKS:(k + 1) * BANK_BLOCKS],
+                           in_=banks[k][:].rearrange("p c n -> p n c"))
+
+        for k in range(len(banks)):
             for c in range(BANK_BLOCKS):
-                col = first + c
-                nc.tensor.transpose(bank[:, c, :], ts_cols[:, col:col + 1].to_broadcast([P, P]), identity[:])
-            nc.scalar.copy(out=ts_view[:, :, first:first + BANK_BLOCKS], in_=bank[:].rearrange("p c n -> p n c"))
+                col = k * BANK_BLOCKS + c
+                nc.tensor.transpose(banks[k][:, c, :], ts_cols[:, col:col + 1].to_broadcast([P, P]), identity[:])
+            if k < len(banks) - 1:
+                empty_bank(k)
 
         def gather_words(b):
             picked = sbuf([P, N], U32, "picked_words_%d" % b)
             nc.vector.tensor_copy(picked[:], word_pool[:].bitcast(U32).indirect(list_of(b)))
             return picked
 
-        def part_words(b, picked, tag=None):
-            keys = sbuf([P, PASSES, 2 * N], U8, "key_words_%d" % b, tag)
+        def part_words(b, picked, offset=None):
+            keys = sbuf([P, PASSES, 2 * N], U8, "key_words_%d" % b, offset=offset)
             nc.vector.tensor_copy(keys[:].bitcast(U16),
                                   picked[:].bitcast(U16).rearrange("p (n o) -> p o n", o=PASSES))
             return keys
 
-        def round_queries(b, o, rounded):
-            nc.scalar.copy(out=rounded.rearrange("p (c i) j -> p c j i", i=4),
-                           in_=q_raw[b, o][:].rearrange("p j (c i) -> p c j i", i=4))
-
-        def quantise(rounded, codes, scales):
-            nc.vector.quantize_mx(out=codes.bitcast(FP8X4), scales=scales, in_=rounded)
+        def round_queries(b, o, copy, offset=None):
+            rounded = sbuf([P, NQ, PACK], BF16, "q_bf_%d_%d" % (b, o), offset=offset)
+            copy(out=rounded[:].rearrange("p (c i) j -> p c j i", i=4),
+                 in_=q_raw[b, o][:].rearrange("p j (c i) -> p c j i", i=4))
+            return rounded
 
         q_codes = [sbuf([P, PASSES, NQ], U32, "q_codes_%d" % b) for b in range(B)]
         q_scales = [sbuf([P, PASSES, NQ], U8, "q_scales_%d" % b) for b in range(B)]
+
+        def quantise(b, o, rounded):
+            nc.vector.quantize_mx(out=q_codes[b][:, o, :].bitcast(FP8X4), scales=q_scales[b][:, o, :],
+                                  in_=rounded[:].rearrange("p q j -> p (q j)"))
 
         def score(b, keys, tag=None):
             acc = psum.tile([NQ, N], F32, name="acc_%d" % b)
@@ -116,7 +129,7 @@ def tile_attend_sddmm_ts_kernel(tc, qT, k_words, k_scales, ts, offs, out):
             return scores
 
         def gather_ts(b):
-            picked_ts = sbuf([P, N], F32, "picked_ts_%d" % b, "slot_b")
+            picked_ts = sbuf([P, N], F32, "picked_ts_%d" % b, "picked_ts")
             nc.vector.tensor_copy(picked_ts[:], ts_pool[:].indirect(list_of(b)))
             return picked_ts
 
@@ -127,16 +140,13 @@ def tile_attend_sddmm_ts_kernel(tc, qT, k_words, k_scales, ts, offs, out):
         picked_words = [gather_words(b) for b in range(B)]
         keys_first = part_words(0, picked_words[0])
         for o in range(PASSES):
-            rounded = sbuf([P, NQ, PACK], BF16, "q_bf_0_%d" % o, "slot_c" if o == PASSES - 1 else None)
-            round_queries(0, o, rounded[:])
-            quantise(rounded[:].rearrange("p q j -> p (q j)"), q_codes[0][:, o, :], q_scales[0][:, o, :])
+            quantise(0, o, round_queries(0, o, nc.scalar.copy, o * KIB))
+        empty_bank(len(banks) - 1)
+        keys_second = part_words(1, picked_words[1], 2 * KIB)
+        rounded = round_queries(1, 0, nc.vector.tensor_copy, 4 * KIB)
         ts_first = gather_ts(0)
-        keys_second = part_words(1, picked_words[1], "slot_c")
-        rounded = sbuf([P, PASSES, NQ, PACK], BF16, "q_bf_1")
-        for o in range(PASSES):
-            round_queries(1, o, rounded[:, o, :, :])
-        quantise(rounded[:].rearrange("p o q j -> p (o q j)"), q_codes[1][:].rearrange("p o q -> p (o q)"),
-                 q_scales[1][:].rearrange("p o q -> p (o q)"))
+        quantise(1, 0, rounded)
+        quantise(1, 1, round_queries(1, 1, nc.scalar.copy))
         scores_first = score(0, keys_first, "slot_a")
         scores_second = score(1, keys_second)
         place(0, scores_first, ts_first)

@@ -48,10 +48,10 @@ def tile_attend_sddmm_ts_kernel(tc, qT, k_words, k_scales, ts, offs, out):
         ts_cols = reused.tile([P, TS_COLS], F32, name="ts_cols", offset=KIB - 32)
         scale_pool = sbuf([P, T], U8, "scale_pool", "slot_a")
         word_pool = sbuf([P, T], I32, "word_pool")
-        nc.sync.dma_start(out=ts_cols[:], in_=ts[0, :].rearrange("(p c) -> p c", c=TS_COLS))
         nc.sync.dma_start(offsets[:], offs)
-        nc.sync.dma_start(out=scale_pool[SCALE_ROW0:P, :].bitcast(I32),
-                          in_=k_scales.rearrange("o f t -> f o t").bitcast(I32))
+        nc.scalar.dma_start(out=scale_pool[SCALE_ROW0:P, :].bitcast(I32),
+                            in_=k_scales.rearrange("o f t -> f o t").bitcast(I32))
+        nc.scalar.dma_start(out=ts_cols[:], in_=ts[0, :].rearrange("(p c) -> p c", c=TS_COLS))
         nc.sync.dma_start(out=word_pool[:], in_=k_words[0].rearrange("p t x -> p (t x)").bitcast(I32))
         q_raw = {(0, 0): load_queries(0, 0), (0, 1): load_queries(0, 1, offset=3 * KIB), (1, 0): load_queries(1, 0)}
 

@@ -46,14 +46,14 @@ def tile_attend_sddmm_ts_kernel(tc, qT, k_words, k_scales, ts, offs, out):
 
         offsets = keep.tile([P, B * LIST_COLS], U16, name="offsets")
         ts_cols = reused.tile([P, TS_COLS], F32, name="ts_cols", offset=KIB - 32)
-        scale_pool = sbuf([P, T], U8, "scale_pool", "slot_a")
+        scale_pool = sbuf([P, T], U8, "scale_pool", offset=8 * KIB)
         word_pool = sbuf([P, T], I32, "word_pool")
         nc.sync.dma_start(offsets[:], offs)
         nc.scalar.dma_start(out=scale_pool[SCALE_ROW0:P, :].bitcast(I32),
                             in_=k_scales.rearrange("o f t -> f o t").bitcast(I32))
         nc.scalar.dma_start(out=ts_cols[:], in_=ts[0, :].rearrange("(p c) -> p c", c=TS_COLS))
         nc.sync.dma_start(out=word_pool[:], in_=k_words[0].rearrange("p t x -> p (t x)").bitcast(I32))
-        q_raw = {(0, 0): load_queries(0, 0), (0, 1): load_queries(0, 1, offset=3 * KIB), (1, 0): load_queries(1, 0)}
+        q_raw = {(0, 0): load_queries(0, 0), (0, 1): load_queries(0, 1, offset=3 * KIB)}
 
         def list_of(b):
             return offsets[:, b * LIST_COLS:(b + 1) * LIST_COLS]
@@ -69,14 +69,21 @@ def tile_attend_sddmm_ts_kernel(tc, qT, k_words, k_scales, ts, offs, out):
         rows.append(sbuf([P, T], F32, "rows_1", "slot_d"))
         nc.gpsimd.memset(rows[1][:].bitcast(I32), 0)
 
-        picked_scales = sbuf([P, B * N], U8, "picked_scales")
-        key_scales = sbuf([P, PASSES, B * N], U8, "key_scales")
-        nc.vector.tensor_copy(picked_scales[:], scale_pool[:].indirect(offsets[:]))
-        for quad in (0, 2, 1, 3):
-            src0 = SCALE_ROW0 + 8 * quad
-            nc.sync.dma_start(out=key_scales[32 * quad:32 * quad + 4, :, :].bitcast(I32),
-                              in_=picked_scales[src0:src0 + 8, :].bitcast(I32))
-        q_raw[1, 1] = load_queries(1, 1, "slot_a")
+        picked_scales = [sbuf([P, N], U8, "picked_scales_%d" % b) for b in range(B)]
+        key_scales = [sbuf([P, PASSES, N], U8, "key_scales_%d" % b) for b in range(B)]
+        for b in range(B):
+            nc.vector.tensor_copy(picked_scales[b][:], scale_pool[:].indirect(list_of(b)))
+
+        def move_scales(b):
+            for quad in (0, 2, 1, 3):
+                src0 = SCALE_ROW0 + 8 * quad
+                nc.sync.dma_start(out=key_scales[b][32 * quad:32 * quad + 4, :, :].bitcast(I32),
+                                  in_=picked_scales[b][src0:src0 + 8, :].bitcast(I32))
+
+        move_scales(0)
+        q_raw[1, 0] = load_queries(1, 0, offset=6 * KIB + 64)
+        q_raw[1, 1] = load_queries(1, 1, offset=10 * KIB - 64)
+        move_scales(1)
 
         ts_pool = sbuf([P, T], F32, "ts_pool")
         ts_view = ts_pool[:].rearrange("p (n c) -> p n c", c=TS_COLS)
@@ -117,14 +124,14 @@ def tile_attend_sddmm_ts_kernel(tc, qT, k_words, k_scales, ts, offs, out):
             nc.vector.quantize_mx(out=q_codes[b][:, o, :].bitcast(FP8X4), scales=q_scales[b][:, o, :],
                                   in_=rounded[:].rearrange("p q j -> p (q j)"))
 
-        def score(b, keys, tag=None):
+        def score(b, keys, offset=None):
             acc = psum.tile([NQ, N], F32, name="acc_%d" % b)
             for o in range(PASSES):
                 nc.tensor.matmul_mx(out=acc[:], lhsT=q_codes[b][:, o, :].bitcast(FP8X4), lhsT_scale=q_scales[b][:, o, :],
                                     rhs=keys[:, o, :].bitcast(FP4X4),
-                                    rhs_scale=key_scales[:, o, b * N:(b + 1) * N],
+                                    rhs_scale=key_scales[b][:, o, :],
                                     start=(o == 0), stop=(o == PASSES - 1))
-            scores = sbuf([P, N], F32, "scores_%d" % b, tag)
+            scores = sbuf([P, N], F32, "scores_%d" % b, offset=offset)
             nc.scalar.copy(out=scores[:], in_=acc[:])
             return scores
 
@@ -143,11 +150,11 @@ def tile_attend_sddmm_ts_kernel(tc, qT, k_words, k_scales, ts, offs, out):
             quantise(0, o, round_queries(0, o, nc.scalar.copy, o * KIB))
         empty_bank(len(banks) - 1)
         keys_second = part_words(1, picked_words[1], 2 * KIB)
-        rounded = round_queries(1, 0, nc.vector.tensor_copy, 4 * KIB)
+        rounded = round_queries(1, 0, nc.scalar.copy)
         ts_first = gather_ts(0)
         quantise(1, 0, rounded)
         quantise(1, 1, round_queries(1, 1, nc.scalar.copy))
-        scores_first = score(0, keys_first, "slot_a")
+        scores_first = score(0, keys_first, 12 * KIB - 128)
         scores_second = score(1, keys_second)
         place(0, scores_first, ts_first)
         place(1, scores_second, gather_ts(1))

@@ -23,6 +23,7 @@ MULT = mybir.AluOpType.mult
 SCALE_ROW0 = 96
 TS_COLS = T // P
 BANK_BLOCKS = 4
+GROUP = 128
 KIB = 1024
 
 
@@ -46,7 +47,7 @@ def tile_attend_sddmm_ts_kernel(tc, qT, k_words, k_scales, ts, offs, out):
 
         offsets = keep.tile([P, B * LIST_COLS], U16, name="offsets")
         ts_cols = reused.tile([P, TS_COLS], F32, name="ts_cols", offset=KIB - 32)
-        scale_pool = sbuf([P, T], U8, "scale_pool", offset=8 * KIB)
+        scale_pool = sbuf([P, T], U8, "scale_pool", offset=12 * KIB)
         word_pool = sbuf([P, T], I32, "word_pool")
         nc.sync.dma_start(offsets[:], offs)
         nc.scalar.dma_start(out=scale_pool[SCALE_ROW0:P, :].bitcast(I32),
@@ -81,13 +82,13 @@ def tile_attend_sddmm_ts_kernel(tc, qT, k_words, k_scales, ts, offs, out):
                                   in_=picked_scales[b][src0:src0 + 8, :].bitcast(I32))
 
         move_scales(0)
-        q_raw[1, 0] = load_queries(1, 0, offset=6 * KIB + 64)
-        q_raw[1, 1] = load_queries(1, 1, offset=10 * KIB - 64)
+        q_raw[1, 0] = load_queries(1, 0, offset=10 * KIB + 64)
+        q_raw[1, 1] = load_queries(1, 1, offset=14 * KIB - 64)
         move_scales(1)
 
         ts_pool = sbuf([P, T], F32, "ts_pool")
         ts_view = ts_pool[:].rearrange("p (n c) -> p n c", c=TS_COLS)
-        banks = [psum.tile([P, BANK_BLOCKS, P], F32, name="ts_bank_%d" % k) for k in range(TS_COLS // BANK_BLOCKS)]
+        banks = [psum.tile([P, BANK_BLOCKS, P], F32, name="ts_bank_%d" % k, tag="ts_bank_%d" % k) for k in range(TS_COLS // BANK_BLOCKS)]
 
         def empty_bank(k):
             nc.scalar.copy(out=ts_view[:, :, k * BANK_BLOCKS:(k + 1) * BANK_BLOCKS],
@@ -111,6 +112,12 @@ def tile_attend_sddmm_ts_kernel(tc, qT, k_words, k_scales, ts, offs, out):
                                   picked[:].bitcast(U16).rearrange("p (n o) -> p o n", o=PASSES))
             return keys
 
+        def part_pass(b, o, picked, offset=None):
+            keys = sbuf([P, 2 * N], U8, "key_words_%d_%d" % (b, o), offset=offset)
+            nc.vector.tensor_copy(keys[:].bitcast(U16),
+                                  picked[:].bitcast(U16).rearrange("p (n o) -> p o n", o=PASSES)[:, o, :])
+            return keys
+
         def round_queries(b, o, copy, offset=None):
             rounded = sbuf([P, NQ, PACK], BF16, "q_bf_%d_%d" % (b, o), offset=offset)
             copy(out=rounded[:].rearrange("p (c i) j -> p c j i", i=4),
@@ -125,7 +132,7 @@ def tile_attend_sddmm_ts_kernel(tc, qT, k_words, k_scales, ts, offs, out):
                                   in_=rounded[:].rearrange("p q j -> p (q j)"))
 
         def score(b, keys, offset=None):
-            acc = psum.tile([NQ, N], F32, name="acc_%d" % b)
+            acc = psum.tile([NQ, N], F32, name="acc_%d" % b, tag="ts_bank_0")
             for o in range(PASSES):
                 nc.tensor.matmul_mx(out=acc[:], lhsT=q_codes[b][:, o, :].bitcast(FP8X4), lhsT_scale=q_scales[b][:, o, :],
                                     rhs=keys[:, o, :].bitcast(FP4X4),
@@ -133,6 +140,20 @@ def tile_attend_sddmm_ts_kernel(tc, qT, k_words, k_scales, ts, offs, out):
                                     start=(o == 0), stop=(o == PASSES - 1))
             scores = sbuf([P, N], F32, "scores_%d" % b, offset=offset)
             nc.scalar.copy(out=scores[:], in_=acc[:])
+            return scores
+
+        def score_in_groups(b, keys, offset):
+            accs = [psum.tile([NQ, GROUP], F32, name="acc_%d_%d" % (b, g)) for g in range(N // GROUP)]
+            for o in range(PASSES):
+                for g, acc in enumerate(accs):
+                    nc.tensor.matmul_mx(out=acc[:], lhsT=q_codes[b][:, o, :].bitcast(FP8X4),
+                                        lhsT_scale=q_scales[b][:, o, :],
+                                        rhs=keys[o][:, 2 * g * GROUP:2 * (g + 1) * GROUP].bitcast(FP4X4),
+                                        rhs_scale=key_scales[b][:, o, g * GROUP:(g + 1) * GROUP],
+                                        start=(o == 0), stop=(o == PASSES - 1))
+            scores = sbuf([P, N], F32, "scores_%d" % b, offset=offset)
+            for g, acc in enumerate(accs):
+                nc.scalar.copy(out=scores[:, g * GROUP:(g + 1) * GROUP], in_=acc[:])
             return scores
 
         def gather_ts(b):
@@ -145,16 +166,18 @@ def tile_attend_sddmm_ts_kernel(tc, qT, k_words, k_scales, ts, offs, out):
             nc.sync.dma_start(out=out[b], in_=rows[b][:])
 
         picked_words = [gather_words(b) for b in range(B)]
-        keys_first = part_words(0, picked_words[0])
-        for o in range(PASSES):
-            quantise(0, o, round_queries(0, o, nc.scalar.copy, o * KIB))
+        keys_first = [part_pass(0, 0, picked_words[0])]
+        quantise(0, 0, round_queries(0, 0, nc.scalar.copy, 0))
+        rounded = round_queries(0, 1, nc.scalar.copy, KIB)
+        keys_first.append(part_pass(0, 1, picked_words[0], 2 * KIB + 64))
+        quantise(0, 1, rounded)
         empty_bank(len(banks) - 1)
-        keys_second = part_words(1, picked_words[1], 2 * KIB)
-        rounded = round_queries(1, 0, nc.scalar.copy)
+        keys_second = part_words(1, picked_words[1], 5 * KIB - 64)
+        rounded = [round_queries(1, 0, nc.scalar.copy, 0), round_queries(1, 1, nc.vector.tensor_copy, 3 * KIB + 64)]
         ts_first = gather_ts(0)
-        quantise(1, 0, rounded)
-        quantise(1, 1, round_queries(1, 1, nc.scalar.copy))
-        scores_first = score(0, keys_first, 12 * KIB - 128)
+        for o in range(PASSES):
+            quantise(1, o, rounded[o])
+        scores_first = score_in_groups(0, keys_first, 8 * KIB + 128)
         scores_second = score(1, keys_second)
         place(0, scores_first, ts_first)
         place(1, scores_second, gather_ts(1))

@@ -59,7 +59,7 @@ def tile_attend_sddmm_ts_kernel(tc, qT, k_words, k_scales, ts, offs, out):
         def list_of(b):
             return offsets[:, b * LIST_COLS:(b + 1) * LIST_COLS]
 
-        zeros = sbuf([P, P], F32, "zeros", "slot_d")
+        zeros = sbuf([P, P], F32, "zeros")
         identity = sbuf([P, P], F32, "identity")
         rows = [sbuf([P, T], F32, "rows_0")]
         nc.vector.memset(zeros[:], 0.0)
@@ -67,13 +67,15 @@ def tile_attend_sddmm_ts_kernel(tc, qT, k_words, k_scales, ts, offs, out):
         nc.vector.memset(rows[0][:].bitcast(I32), 0)
         nc.gpsimd.affine_select(out=identity[:], in_=zeros[:], compare_op=mybir.AluOpType.not_equal, fill=1.0,
                                 base=0, pattern=[[-1, P]], channel_multiplier=1)
-        rows.append(sbuf([P, T], F32, "rows_1", "slot_d"))
-        nc.gpsimd.memset(rows[1][:].bitcast(I32), 0)
+        rows.append(sbuf([P, T], F32, "rows_1"))
+        nc.vector.memset(rows[1][:, :T // 2].bitcast(I32), 0)
 
         picked_scales = [sbuf([P, N], U8, "picked_scales_%d" % b) for b in range(B)]
         key_scales = [sbuf([P, PASSES, N], U8, "key_scales_%d" % b) for b in range(B)]
         for b in range(B):
             nc.vector.tensor_copy(picked_scales[b][:], scale_pool[:].indirect(list_of(b)))
+
+        nc.vector.memset(rows[1][:, T // 2:].bitcast(I32), 0)
 
         def move_scales(b):
             for quad in (0, 2, 1, 3):

@@ -23,6 +23,8 @@ MULT = mybir.AluOpType.mult
 SCALE_ROW0 = 96
 TS_COLS = T // P
 BANK_BLOCKS = 4
+EARLY_BANKS = 2
+EARLY_COLS = 10
 GROUP = 128
 KIB = 1024
 
@@ -72,8 +74,10 @@ def tile_attend_sddmm_ts_kernel(tc, qT, k_words, k_scales, ts, offs, out):
 
         picked_scales = [sbuf([P, N], U8, "picked_scales_%d" % b) for b in range(B)]
         key_scales = [sbuf([P, PASSES, N], U8, "key_scales_%d" % b) for b in range(B)]
-        for b in range(B):
-            nc.vector.tensor_copy(picked_scales[b][:], scale_pool[:].indirect(list_of(b)))
+        ts_late = sbuf([P, TS_COLS - EARLY_COLS], F32, "ts_late")
+        nc.vector.tensor_copy(picked_scales[0][:], scale_pool[:].indirect(list_of(0)))
+        nc.vector.tensor_copy(ts_late[:], ts_cols[:, EARLY_COLS:])
+        nc.vector.tensor_copy(picked_scales[1][:], scale_pool[:].indirect(list_of(1)))
 
         nc.vector.memset(rows[1][:, T // 2:].bitcast(I32), 0)
 
@@ -99,8 +103,9 @@ def tile_attend_sddmm_ts_kernel(tc, qT, k_words, k_scales, ts, offs, out):
         for k in range(len(banks)):
             for c in range(BANK_BLOCKS):
                 col = k * BANK_BLOCKS + c
-                nc.tensor.transpose(banks[k][:, c, :], ts_cols[:, col:col + 1].to_broadcast([P, P]), identity[:])
-            if k < len(banks) - 1:
+                column = ts_cols[:, col:col + 1] if col < EARLY_COLS else ts_late[:, col - EARLY_COLS:col - EARLY_COLS + 1]
+                nc.tensor.transpose(banks[k][:, c, :], column.to_broadcast([P, P]), identity[:])
+            if k < EARLY_BANKS:
                 empty_bank(k)
 
         def gather_words(b):
@@ -173,7 +178,8 @@ def tile_attend_sddmm_ts_kernel(tc, qT, k_words, k_scales, ts, offs, out):
         rounded = round_queries(0, 1, nc.scalar.copy, KIB)
         keys_first.append(part_pass(0, 1, picked_words[0], 2 * KIB + 64))
         quantise(0, 1, rounded)
-        empty_bank(len(banks) - 1)
+        for k in range(EARLY_BANKS, len(banks)):
+            empty_bank(k)
         keys_second = part_words(1, picked_words[1], 5 * KIB - 64)
         rounded = [round_queries(1, 0, nc.scalar.copy, 0), round_queries(1, 1, nc.vector.tensor_copy, 3 * KIB + 64)]
         ts_first = gather_ts(0)

@@ -23,8 +23,8 @@ MULT = mybir.AluOpType.mult
 SCALE_ROW0 = 96
 TS_COLS = T // P
 BANK_BLOCKS = 4
-EARLY_BANKS = 2
-EARLY_COLS = 10
+EARLY_BANKS = 3
+EARLY_COLS = 14
 GROUP = 128
 KIB = 1024
 
@@ -52,11 +52,11 @@ def tile_attend_sddmm_ts_kernel(tc, qT, k_words, k_scales, ts, offs, out):
         scale_pool = sbuf([P, T], U8, "scale_pool", offset=12 * KIB)
         word_pool = sbuf([P, T], I32, "word_pool")
         nc.sync.dma_start(offsets[:], offs)
+        nc.scalar.dma_start(out=ts_cols[:], in_=ts[0, :].rearrange("(p c) -> p c", c=TS_COLS))
         nc.scalar.dma_start(out=scale_pool[SCALE_ROW0:P, :].bitcast(I32),
                             in_=k_scales.rearrange("o f t -> f o t").bitcast(I32))
-        nc.scalar.dma_start(out=ts_cols[:], in_=ts[0, :].rearrange("(p c) -> p c", c=TS_COLS))
         nc.sync.dma_start(out=word_pool[:], in_=k_words[0].rearrange("p t x -> p (t x)").bitcast(I32))
-        q_raw = {(0, 0): load_queries(0, 0), (0, 1): load_queries(0, 1, offset=3 * KIB)}
+        q_raw = {(0, 0): load_queries(0, 0, offset=20 * KIB), (0, 1): load_queries(0, 1, offset=3 * KIB)}
 
         def list_of(b):
             return offsets[:, b * LIST_COLS:(b + 1) * LIST_COLS]
@@ -125,10 +125,10 @@ def tile_attend_sddmm_ts_kernel(tc, qT, k_words, k_scales, ts, offs, out):
                                   picked[:].bitcast(U16).rearrange("p (n o) -> p o n", o=PASSES)[:, o, :])
             return keys
 
-        def round_queries(b, o, copy, offset=None):
+        def round_queries(b, o, offset=None):
             rounded = sbuf([P, NQ, PACK], BF16, "q_bf_%d_%d" % (b, o), offset=offset)
-            copy(out=rounded[:].rearrange("p (c i) j -> p c j i", i=4),
-                 in_=q_raw[b, o][:].rearrange("p j (c i) -> p c j i", i=4))
+            nc.scalar.copy(out=rounded[:].rearrange("p (c i) j -> p c j i", i=4),
+                           in_=q_raw[b, o][:].rearrange("p j (c i) -> p c j i", i=4))
             return rounded
 
         q_codes = [sbuf([P, PASSES, NQ], U32, "q_codes_%d" % b) for b in range(B)]
@@ -138,19 +138,9 @@ def tile_attend_sddmm_ts_kernel(tc, qT, k_words, k_scales, ts, offs, out):
             nc.vector.quantize_mx(out=q_codes[b][:, o, :].bitcast(FP8X4), scales=q_scales[b][:, o, :],
                                   in_=rounded[:].rearrange("p q j -> p (q j)"))
 
-        def score(b, keys, offset=None):
-            acc = psum.tile([NQ, N], F32, name="acc_%d" % b, tag="ts_bank_0")
-            for o in range(PASSES):
-                nc.tensor.matmul_mx(out=acc[:], lhsT=q_codes[b][:, o, :].bitcast(FP8X4), lhsT_scale=q_scales[b][:, o, :],
-                                    rhs=keys[:, o, :].bitcast(FP4X4),
-                                    rhs_scale=key_scales[b][:, o, :],
-                                    start=(o == 0), stop=(o == PASSES - 1))
-            scores = sbuf([P, N], F32, "scores_%d" % b, offset=offset)
-            nc.scalar.copy(out=scores[:], in_=acc[:])
-            return scores
-
-        def score_in_groups(b, keys, offset):
-            accs = [psum.tile([NQ, GROUP], F32, name="acc_%d_%d" % (b, g)) for g in range(N // GROUP)]
+        def score_in_groups(b, keys, offset=None):
+            accs = [psum.tile([NQ, GROUP], F32, name="acc_%d_%d" % (b, g), tag=("acc_%d" if b == 0 else "ts_bank_%d") % g)
+                    for g in range(N // GROUP)]
             for o in range(PASSES):
                 for g, acc in enumerate(accs):
                     nc.tensor.matmul_mx(out=acc[:], lhsT=q_codes[b][:, o, :].bitcast(FP8X4),
@@ -163,8 +153,8 @@ def tile_attend_sddmm_ts_kernel(tc, qT, k_words, k_scales, ts, offs, out):
                 nc.scalar.copy(out=scores[:, g * GROUP:(g + 1) * GROUP], in_=acc[:])
             return scores
 
-        def gather_ts(b):
-            picked_ts = sbuf([P, N], F32, "picked_ts_%d" % b, "picked_ts")
+        def gather_ts(b, offset=None):
+            picked_ts = sbuf([P, N], F32, "picked_ts_%d" % b, offset=offset)
             nc.vector.tensor_copy(picked_ts[:], ts_pool[:].indirect(list_of(b)))
             return picked_ts
 
@@ -174,18 +164,18 @@ def tile_attend_sddmm_ts_kernel(tc, qT, k_words, k_scales, ts, offs, out):
 
         picked_words = [gather_words(b) for b in range(B)]
         keys_first = [part_pass(0, 0, picked_words[0])]
-        quantise(0, 0, round_queries(0, 0, nc.scalar.copy, 0))
-        rounded = round_queries(0, 1, nc.scalar.copy, KIB)
-        keys_first.append(part_pass(0, 1, picked_words[0], 2 * KIB + 64))
+        quantise(0, 0, round_queries(0, 0, 0))
+        rounded = round_queries(0, 1, KIB)
+        keys_first.append(part_pass(0, 1, picked_words[0], 19 * KIB + 64))
         quantise(0, 1, rounded)
         for k in range(EARLY_BANKS, len(banks)):
             empty_bank(k)
         keys_second = part_words(1, picked_words[1], 5 * KIB - 64)
-        rounded = [round_queries(1, 0, nc.scalar.copy, 0), round_queries(1, 1, nc.vector.tensor_copy, 3 * KIB + 64)]
         ts_first = gather_ts(0)
-        for o in range(PASSES):
-            quantise(1, o, rounded[o])
+        quantise(1, 0, round_queries(1, 0, 0))
         scores_first = score_in_groups(0, keys_first, 8 * KIB + 128)
-        scores_second = score(1, keys_second)
         place(0, scores_first, ts_first)
-        place(1, scores_second, gather_ts(1))
+        quantise(1, 1, round_queries(1, 1, 11 * KIB))
+        ts_second = gather_ts(1, 16 * KIB - 128)
+        scores_second = score_in_groups(1, [keys_second[:, o, :] for o in range(PASSES)])
+        place(1, scores_second, ts_second)

@@ -138,7 +138,7 @@ def tile_attend_sddmm_ts_kernel(tc, qT, k_words, k_scales, ts, offs, out):
             nc.vector.quantize_mx(out=q_codes[b][:, o, :].bitcast(FP8X4), scales=q_scales[b][:, o, :],
                                   in_=rounded[:].rearrange("p q j -> p (q j)"))
 
-        def score_in_groups(b, keys, offset=None):
+        def score_in_groups(b, keys, offset=None, warm_with=None):
             accs = [psum.tile([NQ, GROUP], F32, name="acc_%d_%d" % (b, g), tag=("acc_%d" if b == 0 else "ts_bank_%d") % g)
                     for g in range(N // GROUP)]
             for o in range(PASSES):
@@ -148,6 +148,11 @@ def tile_attend_sddmm_ts_kernel(tc, qT, k_words, k_scales, ts, offs, out):
                                         rhs=keys[o][:, 2 * g * GROUP:2 * (g + 1) * GROUP].bitcast(FP4X4),
                                         rhs_scale=key_scales[b][:, o, g * GROUP:(g + 1) * GROUP],
                                         start=(o == 0), stop=(o == PASSES - 1))
+                if warm_with is not None and o == 0:
+                    spare = psum.tile([NQ, N], F32, name="spare", tag="acc_0")
+                    nc.tensor.matmul_mx(out=spare[:], lhsT=q_codes[b][:, o, :].bitcast(FP8X4),
+                                        lhsT_scale=q_scales[b][:, o, :], rhs=warm_with.bitcast(FP4X4),
+                                        rhs_scale=key_scales[b][:, o, :], start=True, stop=True)
             scores = sbuf([P, N], F32, "scores_%d" % b, offset=offset)
             for g, acc in enumerate(accs):
                 nc.scalar.copy(out=scores[:, g * GROUP:(g + 1) * GROUP], in_=acc[:])
@@ -177,5 +182,5 @@ def tile_attend_sddmm_ts_kernel(tc, qT, k_words, k_scales, ts, offs, out):
         place(0, scores_first, ts_first)
         quantise(1, 1, round_queries(1, 1, 11 * KIB))
         ts_second = gather_ts(1, 16 * KIB - 128)
-        scores_second = score_in_groups(1, [keys_second[:, o, :] for o in range(PASSES)])
+        scores_second = score_in_groups(1, [keys_second[:, o, :] for o in range(PASSES)], None, keys_second[:, 0, :])
         place(1, scores_second, ts_second)

@@ -56,7 +56,7 @@ def tile_attend_sddmm_ts_kernel(tc, qT, k_words, k_scales, ts, offs, out):
         nc.scalar.dma_start(out=scale_pool[SCALE_ROW0:P, :].bitcast(I32),
                             in_=k_scales.rearrange("o f t -> f o t").bitcast(I32))
         nc.sync.dma_start(out=word_pool[:], in_=k_words[0].rearrange("p t x -> p (t x)").bitcast(I32))
-        q_raw = {(0, 0): load_queries(0, 0, offset=20 * KIB), (0, 1): load_queries(0, 1, offset=3 * KIB)}
+        q_raw = {(0, 0): load_queries(0, 0, offset=20 * KIB), (0, 1): load_queries(0, 1, offset=24 * KIB)}
 
         def list_of(b):
             return offsets[:, b * LIST_COLS:(b + 1) * LIST_COLS]
@@ -125,20 +125,20 @@ def tile_attend_sddmm_ts_kernel(tc, qT, k_words, k_scales, ts, offs, out):
                                   picked[:].bitcast(U16).rearrange("p (n o) -> p o n", o=PASSES)[:, o, :])
             return keys
 
-        def round_queries(b, o, offset=None):
+        def round_queries(b, o, offset=None, copy=nc.scalar.copy):
             rounded = sbuf([P, NQ, PACK], BF16, "q_bf_%d_%d" % (b, o), offset=offset)
-            nc.scalar.copy(out=rounded[:].rearrange("p (c i) j -> p c j i", i=4),
-                           in_=q_raw[b, o][:].rearrange("p j (c i) -> p c j i", i=4))
+            copy(out=rounded[:].rearrange("p (c i) j -> p c j i", i=4),
+                 in_=q_raw[b, o][:].rearrange("p j (c i) -> p c j i", i=4))
             return rounded
 
         q_codes = [sbuf([P, PASSES, NQ], U32, "q_codes_%d" % b) for b in range(B)]
-        q_scales = [sbuf([P, PASSES, NQ], U8, "q_scales_%d" % b) for b in range(B)]
+        q_scales = [sbuf([P, PASSES, NQ], U8, "q_scales_0"), sbuf([P, PASSES, NQ], U8, "q_scales_1", offset=10 * KIB + 256)]
 
         def quantise(b, o, rounded):
             nc.vector.quantize_mx(out=q_codes[b][:, o, :].bitcast(FP8X4), scales=q_scales[b][:, o, :],
                                   in_=rounded[:].rearrange("p q j -> p (q j)"))
 
-        def score_in_groups(b, keys, offset=None, warm_with=None):
+        def score_in_groups(b, keys, offset=None):
             accs = [psum.tile([NQ, GROUP], F32, name="acc_%d_%d" % (b, g), tag=("acc_%d" if b == 0 else "ts_bank_%d") % g)
                     for g in range(N // GROUP)]
             for o in range(PASSES):
@@ -148,11 +148,6 @@ def tile_attend_sddmm_ts_kernel(tc, qT, k_words, k_scales, ts, offs, out):
                                         rhs=keys[o][:, 2 * g * GROUP:2 * (g + 1) * GROUP].bitcast(FP4X4),
                                         rhs_scale=key_scales[b][:, o, g * GROUP:(g + 1) * GROUP],
                                         start=(o == 0), stop=(o == PASSES - 1))
-                if warm_with is not None and o == 0:
-                    spare = psum.tile([NQ, N], F32, name="spare", tag="acc_0")
-                    nc.tensor.matmul_mx(out=spare[:], lhsT=q_codes[b][:, o, :].bitcast(FP8X4),
-                                        lhsT_scale=q_scales[b][:, o, :], rhs=warm_with.bitcast(FP4X4),
-                                        rhs_scale=key_scales[b][:, o, :], start=True, stop=True)
             scores = sbuf([P, N], F32, "scores_%d" % b, offset=offset)
             for g, acc in enumerate(accs):
                 nc.scalar.copy(out=scores[:, g * GROUP:(g + 1) * GROUP], in_=acc[:])
@@ -175,12 +170,13 @@ def tile_attend_sddmm_ts_kernel(tc, qT, k_words, k_scales, ts, offs, out):
         quantise(0, 1, rounded)
         for k in range(EARLY_BANKS, len(banks)):
             empty_bank(k)
-        keys_second = part_words(1, picked_words[1], 5 * KIB - 64)
+        keys_second = part_words(1, picked_words[1], 26 * KIB - 64)
         ts_first = gather_ts(0)
-        quantise(1, 0, round_queries(1, 0, 0))
+        rounded = [round_queries(1, 0, 0), round_queries(1, 1, 11 * KIB, nc.vector.tensor_copy)]
+        for o in range(PASSES):
+            quantise(1, o, rounded[o])
         scores_first = score_in_groups(0, keys_first, 8 * KIB + 128)
         place(0, scores_first, ts_first)
-        quantise(1, 1, round_queries(1, 1, 11 * KIB))
-        ts_second = gather_ts(1, 16 * KIB - 128)
-        scores_second = score_in_groups(1, [keys_second[:, o, :] for o in range(PASSES)], None, keys_second[:, 0, :])
+        ts_second = gather_ts(1, 6 * KIB + 192)
+        scores_second = score_in_groups(1, [keys_second[:, o, :] for o in range(PASSES)])
         place(1, scores_second, ts_second)

@@ -113,17 +113,11 @@ def tile_attend_sddmm_ts_kernel(tc, qT, k_words, k_scales, ts, offs, out):
             nc.vector.tensor_copy(picked[:], word_pool[:].bitcast(U32).indirect(list_of(b)))
             return picked
 
-        def part_words(b, picked, offset=None):
-            keys = sbuf([P, PASSES, 2 * N], U8, "key_words_%d" % b, offset=offset)
+        def part_pass(b, o, picked, offset=None, first=0, count=N):
+            keys = sbuf([P, 2 * count], U8, "key_words_%d_%d_%d" % (b, o, first), offset=offset)
             nc.vector.tensor_copy(keys[:].bitcast(U16),
-                                  picked[:].bitcast(U16).rearrange("p (n o) -> p o n", o=PASSES))
-            return keys
-
-        def part_pass(b, o, picked, offset=None):
-            keys = sbuf([P, 2 * N], U8, "key_words_%d_%d" % (b, o), offset=offset)
-            nc.vector.tensor_copy(keys[:].bitcast(U16),
-                                  picked[:].bitcast(U16).rearrange("p (n o) -> p o n", o=PASSES)[:, o, :])
-            return keys
+                                  picked[:].bitcast(U16).rearrange("p (n o) -> p o n", o=PASSES)[:, o, first:first + count])
+            return [keys[:, 2 * g * GROUP:2 * (g + 1) * GROUP] for g in range(count // GROUP)]
 
         def round_queries(b, o, offset=None, copy=nc.scalar.copy):
             rounded = sbuf([P, NQ, PACK], BF16, "q_bf_%d_%d" % (b, o), offset=offset)
@@ -145,7 +139,7 @@ def tile_attend_sddmm_ts_kernel(tc, qT, k_words, k_scales, ts, offs, out):
                 for g, acc in enumerate(accs):
                     nc.tensor.matmul_mx(out=acc[:], lhsT=q_codes[b][:, o, :].bitcast(FP8X4),
                                         lhsT_scale=q_scales[b][:, o, :],
-                                        rhs=keys[o][:, 2 * g * GROUP:2 * (g + 1) * GROUP].bitcast(FP4X4),
+                                        rhs=keys[o][g].bitcast(FP4X4),
                                         rhs_scale=key_scales[b][:, o, g * GROUP:(g + 1) * GROUP],
                                         start=(o == 0), stop=(o == PASSES - 1))
             scores = sbuf([P, N], F32, "scores_%d" % b, offset=offset)
@@ -170,13 +164,15 @@ def tile_attend_sddmm_ts_kernel(tc, qT, k_words, k_scales, ts, offs, out):
         quantise(0, 1, rounded)
         for k in range(EARLY_BANKS, len(banks)):
             empty_bank(k)
-        keys_second = part_words(1, picked_words[1], 26 * KIB - 64)
+        keys_second = [part_pass(1, 0, picked_words[1], 26 * KIB - 64),
+                       part_pass(1, 1, picked_words[1], 24 * KIB - 448, 0, N // 2)]
         ts_first = gather_ts(0)
         rounded = [round_queries(1, 0, 0), round_queries(1, 1, 11 * KIB, nc.vector.tensor_copy)]
         for o in range(PASSES):
             quantise(1, o, rounded[o])
         scores_first = score_in_groups(0, keys_first, 8 * KIB + 128)
         place(0, scores_first, ts_first)
+        keys_second[1].extend(part_pass(1, 1, picked_words[1], 11 * KIB + 512, N // 2, N // 2))
         ts_second = gather_ts(1, 6 * KIB + 192)
-        scores_second = score_in_groups(1, [keys_second[:, o, :] for o in range(PASSES)])
+        scores_second = score_in_groups(1, keys_second)
         place(1, scores_second, ts_second)

from contextlib import ExitStack

import concourse.mybir as mybir

B, N, T, D, NQ = 2, 512, 2048, 1024, 128
P = 128
PACK = 4
K_PASS = P * PACK
PASSES = D // K_PASS
LIST_COLS = N // 16
FLOPS = 2 * B * NQ * N * D

F32 = mybir.dt.float32
BF16 = mybir.dt.bfloat16
I32 = mybir.dt.int32
U32 = mybir.dt.uint32
U16 = mybir.dt.uint16
U8 = mybir.dt.uint8
FP8X4 = mybir.dt.float8_e4m3fn_x4
FP4X4 = mybir.dt.float4_e2m1fn_x4
MULT = mybir.AluOpType.mult

SCALE_ROW0 = 96
TS_COLS = T // P
BANK_BLOCKS = 4
EARLY_BANKS = 3
EARLY_COLS = 14
GROUP = 128
KIB = 1024


def tile_attend_sddmm_ts_kernel(tc, qT, k_words, k_scales, ts, offs, out):
    nc = tc.nc
    with ExitStack() as ctx:
        keep = ctx.enter_context(tc.tile_pool(name="keep", bufs=1))
        reused = ctx.enter_context(tc.tile_pool(name="reused", bufs=1))
        psum = ctx.enter_context(tc.psum_pool(name="psum", bufs=1))

        def sbuf(shape, dtype, name, tag=None, offset=None):
            if offset is not None:
                return reused.tile(shape, dtype, name=name, align_bytes=64, offset=offset)
            return keep.tile(shape, dtype, name=name, tag=tag or name, align_bytes=64)

        def load_queries(b, o, tag=None, offset=None):
            raw = sbuf([P, PACK, NQ], F32, "q_raw_%d_%d" % (b, o), tag, offset)
            nc.sync.dma_start(out=raw[:],
                              in_=qT[b, o * K_PASS:(o + 1) * K_PASS, :].rearrange("(p j) q -> p j q", j=PACK))
            return raw

        offsets = keep.tile([P, B * LIST_COLS], U16, name="offsets")
        ts_cols = reused.tile([P, TS_COLS], F32, name="ts_cols", offset=KIB - 32)
        scale_pool = sbuf([P, T], U8, "scale_pool", offset=12 * KIB)
        word_pool = sbuf([P, T], I32, "word_pool")
        nc.sync.dma_start(offsets[:], offs)
        nc.scalar.dma_start(out=ts_cols[:], in_=ts[0, :].rearrange("(p c) -> p c", c=TS_COLS))
        nc.scalar.dma_start(out=scale_pool[SCALE_ROW0:P, :].bitcast(I32),
                            in_=k_scales.rearrange("o f t -> f o t").bitcast(I32))
        nc.sync.dma_start(out=word_pool[:], in_=k_words[0].rearrange("p t x -> p (t x)").bitcast(I32))
        q_raw = {(0, 0): load_queries(0, 0, offset=20 * KIB), (0, 1): load_queries(0, 1, offset=24 * KIB)}

        def list_of(b):
            return offsets[:, b * LIST_COLS:(b + 1) * LIST_COLS]

        zeros = sbuf([P, P], F32, "zeros")
        identity = sbuf([P, P], F32, "identity")
        rows = [sbuf([P, T], F32, "rows_0")]
        nc.vector.memset(zeros[:], 0.0)
        nc.vector.memset(scale_pool[0:SCALE_ROW0, :].bitcast(I32), 0)
        nc.vector.memset(rows[0][:].bitcast(I32), 0)
        nc.gpsimd.affine_select(out=identity[:], in_=zeros[:], compare_op=mybir.AluOpType.not_equal, fill=1.0,
                                base=0, pattern=[[-1, P]], channel_multiplier=1)
        rows.append(sbuf([P, T], F32, "rows_1"))
        nc.vector.memset(rows[1][:, :T // 2].bitcast(I32), 0)

        picked_scales = [sbuf([P, N], U8, "picked_scales_%d" % b) for b in range(B)]
        key_scales = [sbuf([P, PASSES, N], U8, "key_scales_%d" % b) for b in range(B)]
        ts_late = sbuf([P, TS_COLS - EARLY_COLS], F32, "ts_late")
        nc.vector.tensor_copy(picked_scales[0][:], scale_pool[:].indirect(list_of(0)))
        nc.vector.tensor_copy(ts_late[:], ts_cols[:, EARLY_COLS:])
        nc.vector.tensor_copy(picked_scales[1][:], scale_pool[:].indirect(list_of(1)))

        nc.vector.memset(rows[1][:, T // 2:].bitcast(I32), 0)

        def move_scales(b):
            for quad in (0, 2, 1, 3):
                src0 = SCALE_ROW0 + 8 * quad
                nc.sync.dma_start(out=key_scales[b][32 * quad:32 * quad + 4, :, :].bitcast(I32),
                                  in_=picked_scales[b][src0:src0 + 8, :].bitcast(I32))

        move_scales(0)
        q_raw[1, 0] = load_queries(1, 0, offset=10 * KIB + 64)
        q_raw[1, 1] = load_queries(1, 1, offset=14 * KIB - 64)
        move_scales(1)

        ts_pool = sbuf([P, T], F32, "ts_pool")
        ts_view = ts_pool[:].rearrange("p (n c) -> p n c", c=TS_COLS)
        banks = [psum.tile([P, BANK_BLOCKS, P], F32, name="ts_bank_%d" % k, tag="ts_bank_%d" % k) for k in range(TS_COLS // BANK_BLOCKS)]

        def empty_bank(k):
            nc.scalar.copy(out=ts_view[:, :, k * BANK_BLOCKS:(k + 1) * BANK_BLOCKS],
                           in_=banks[k][:].rearrange("p c n -> p n c"))

        for k in range(len(banks)):
            for c in range(BANK_BLOCKS):
                col = k * BANK_BLOCKS + c
                column = ts_cols[:, col:col + 1] if col < EARLY_COLS else ts_late[:, col - EARLY_COLS:col - EARLY_COLS + 1]
                nc.tensor.transpose(banks[k][:, c, :], column.to_broadcast([P, P]), identity[:])
            if k < EARLY_BANKS:
                empty_bank(k)

        def gather_words(b):
            picked = sbuf([P, N], U32, "picked_words_%d" % b)
            nc.vector.tensor_copy(picked[:], word_pool[:].bitcast(U32).indirect(list_of(b)))
            return picked

        def part_pass(b, o, picked, offset=None, first=0, count=N):
            keys = sbuf([P, 2 * count], U8, "key_words_%d_%d_%d" % (b, o, first), offset=offset)
            nc.vector.tensor_copy(keys[:].bitcast(U16),
                                  picked[:].bitcast(U16).rearrange("p (n o) -> p o n", o=PASSES)[:, o, first:first + count])
            return [keys[:, 2 * g * GROUP:2 * (g + 1) * GROUP] for g in range(count // GROUP)]

        def round_queries(b, o, offset=None, copy=nc.scalar.copy):
            rounded = sbuf([P, NQ, PACK], BF16, "q_bf_%d_%d" % (b, o), offset=offset)
            copy(out=rounded[:].rearrange("p (c i) j -> p c j i", i=4),
                 in_=q_raw[b, o][:].rearrange("p j (c i) -> p c j i", i=4))
            return rounded

        q_codes = [sbuf([P, PASSES, NQ], U32, "q_codes_%d" % b) for b in range(B)]
        q_scales = [sbuf([P, PASSES, NQ], U8, "q_scales_0"), sbuf([P, PASSES, NQ], U8, "q_scales_1", offset=10 * KIB + 256)]

        def quantise(b, o, rounded):
            nc.vector.quantize_mx(out=q_codes[b][:, o, :].bitcast(FP8X4), scales=q_scales[b][:, o, :],
                                  in_=rounded[:].rearrange("p q j -> p (q j)"))

        def score_in_groups(b, keys, offset=None):
            accs = [psum.tile([NQ, GROUP], F32, name="acc_%d_%d" % (b, g), tag=("acc_%d" if b == 0 else "ts_bank_%d") % g)
                    for g in range(N // GROUP)]
            for o in range(PASSES):
                for g, acc in enumerate(accs):
                    nc.tensor.matmul_mx(out=acc[:], lhsT=q_codes[b][:, o, :].bitcast(FP8X4),
                                        lhsT_scale=q_scales[b][:, o, :],
                                        rhs=keys[o][g].bitcast(FP4X4),
                                        rhs_scale=key_scales[b][:, o, g * GROUP:(g + 1) * GROUP],
                                        start=(o == 0), stop=(o == PASSES - 1))
            scores = sbuf([P, N], F32, "scores_%d" % b, offset=offset)
            for g, acc in enumerate(accs):
                nc.scalar.copy(out=scores[:, g * GROUP:(g + 1) * GROUP], in_=acc[:])
            return scores

        def gather_ts(b, offset=None):
            picked_ts = sbuf([P, N], F32, "picked_ts_%d" % b, offset=offset)
            nc.vector.tensor_copy(picked_ts[:], ts_pool[:].indirect(list_of(b)))
            return picked_ts

        def place(b, scores, picked_ts):
            nc.vector.tensor_tensor(rows[b][:].indirect(list_of(b)), scores[:], picked_ts[:], MULT)
            nc.sync.dma_start(out=out[b], in_=rows[b][:])

        picked_words = [gather_words(b) for b in range(B)]
        keys_first = [part_pass(0, 0, picked_words[0])]
        quantise(0, 0, round_queries(0, 0, 0))
        rounded = round_queries(0, 1, KIB)
        keys_first.append(part_pass(0, 1, picked_words[0], 19 * KIB + 64))
        quantise(0, 1, rounded)
        for k in range(EARLY_BANKS, len(banks)):
            empty_bank(k)
        keys_second = [part_pass(1, 0, picked_words[1], 26 * KIB - 64),
                       part_pass(1, 1, picked_words[1], 24 * KIB - 448, 0, N // 2)]
        ts_first = gather_ts(0)
        rounded = [round_queries(1, 0, 0), round_queries(1, 1, 11 * KIB, nc.vector.tensor_copy)]
        for o in range(PASSES):
            quantise(1, o, rounded[o])
        scores_first = score_in_groups(0, keys_first, 8 * KIB + 128)
        place(0, scores_first, ts_first)
        keys_second[1].extend(part_pass(1, 1, picked_words[1], 11 * KIB + 512, N // 2, N // 2))
        ts_second = gather_ts(1, 6 * KIB + 192)
        scores_second = score_in_groups(1, keys_second)
        place(1, scores_second, ts_second)
